import numpy as np
import ml_dtypes


def mxq(x, axis, fmt="e4m3"):
    dtype, down = {"e4m3": (ml_dtypes.float8_e4m3fn, 7), "e5m2": (ml_dtypes.float8_e5m2, 14)}[fmt]
    v = np.moveaxis(np.asarray(x, np.float32).astype(ml_dtypes.bfloat16).astype(np.float64), axis, -1)
    blocks = v.reshape(v.shape[:-1] + (-1, 32))
    amax = np.abs(blocks).max(-1, keepdims=True)
    byte = np.maximum(np.where(amax > 0, np.frexp(amax)[1] - 1 + 127, 0) - down, 1)
    scale = np.exp2(byte - 127.0)
    codes = (blocks / scale).astype(np.float32).astype(dtype).astype(np.float64)
    return np.moveaxis((codes * scale).reshape(v.shape), -1, axis)


WIDE = False


def mx_kscale(k, group=512):
    if not WIDE:
        return np.ones(k)
    levels = np.array([10, -10, 5, -5, 0])
    if group != 512:
        return np.exp2(np.random.permutation(np.resize(levels, k // group))).repeat(group)
    if k % 512:
        return np.exp2(np.random.permutation(np.resize(levels, k // 32))).repeat(32)
    a = np.empty((k // 512, 16))
    for p in range(k // 512):
        a[p, :8] = np.random.permutation(np.resize(levels, 8))
        for g in range(8):
            far = levels[np.abs(levels - a[p, g]) >= 10]
            a[p, g + 8] = far[np.random.randint(len(far))]
    return np.exp2(a.ravel()).repeat(32)


def f64(x):
    return np.asarray(x).astype(np.float64)


def striped(idx):
    return np.tile(np.asarray(idx).reshape(-1, 16).T, (8, 1)).astype(np.uint16)


def unstriped(offs):
    return offs[:16].T.reshape(-1).astype(np.int64)


H, KV, D, NQ, N = 4, 1, 256, 512, 1024


def setup_inputs():
    n = np.random.standard_normal
    s = mx_kscale(D, 0)[:, None]
    u = mx_kscale(N)
    t = np.random.uniform(0.5, 2.0, N) * u
    v = n((KV, N, 128))
    v[:, :, 127] = 1.0
    return {
        "qT": (n((H, D, NQ)) * s * (0.70 / np.sqrt(D))).astype(np.float32),
        "kT": (n((KV, D, N)) / s).astype(np.float32),
        "t": t.reshape(N, 1).astype(np.float32),
        "v": (v / t[:, None]).astype(np.float32),
    }


def reference(qT, kT, t, v):
    a = np.repeat(mxq(f64(kT), 1, "e4m3"), H // KV, 0).transpose(0, 2, 1) @ mxq(f64(qT), 1, "e4m3")
    p = np.exp(a)
    w = p * f64(t)
    y = mxq(w, 1, "e4m3").transpose(0, 2, 1) @ np.repeat(mxq(f64(v), 1, "e4m3"), H // KV, 0)
    y = y / (y[:, :, 127:128])
    return y

from contextlib import ExitStack

import concourse.mybir as mybir

H, D, NQ, N, E = 4, 256, 512, 1024, 128
FLOPS = 2 * H * N * NQ * (D + E)

F32 = mybir.dt.float32
BF16 = mybir.dt.bfloat16
I32 = mybir.dt.int32
U8 = mybir.dt.uint8
FP8X4 = mybir.dt.float8_e4m3fn_x4
ALU = mybir.AluOpType
ACT = mybir.ActivationFunctionType

P = 128
ROWS = 64
PACK = 4
PASS = 512
COLS = 128
HALF = NQ // 2
SCORE_BANKS = 3
AHEAD = 2
TAIL = 0
PV_UNITS = 2
VECTOR_HEADS = 1
DIV_DELAY = 3
V_SLOT = 1
QC_SLOT = 7
LN_MIN, LN_MAX = 2.0 ** -64, 2.0 ** 64
F32_MIN = 2.0 ** -126


def tile_rows_gqa_kernel(tc, qT, kT, t, v, out):
    nc = tc.nc
    with ExitStack() as ctx:
        sb = ctx.enter_context(tc.tile_pool(name="sb", bufs=1))
        score_pools = [ctx.enter_context(tc.psum_pool(name="scores%d" % T, bufs=SCORE_BANKS)) for T in range(2)]
        y_pool = ctx.enter_context(tc.psum_pool(name="ysum", bufs=2))
        ctx.enter_context(tc.manual_schedule())

        def tile(name, shape, dtype):
            return sb.tile(shape, dtype, name=name, align_bytes=64)

        def quantize(name, grouped, width):
            codes = tile(name + "_codes", [P, width], I32)
            scales = tile(name + "_scales", [P, width], U8)
            nc.vector.quantize_mx(out=codes[:].bitcast(FP8X4), scales=scales[:], in_=grouped)
            return codes, scales

        def interleave(name, rows, width):
            grouped = tile(name + "_grouped", [P, width * PACK], BF16)
            nc.vector.tensor_copy(
                out=grouped[:].rearrange("p (c i j) -> p c j i", i=4, j=PACK),
                in_=rows.rearrange("p j (c i) -> p c j i", i=4),
            )
            return grouped[:]

        t_sb = tile("t_sb", [P, 2, PACK], F32)
        nc.sync.dma_start(out=t_sb[:], in_=t.rearrange("(g p j) o -> p g (j o)", g=2, j=PACK))
        k_raw = tile("k_raw", [P, PACK, PASS], F32)
        k_rows = kT[0].rearrange("(p j) n -> p j n", j=PACK)
        nc.sync.dma_start(out=k_raw[0:ROWS], in_=k_rows[:, :, 0:PASS])
        nc.scalar.dma_start(out=k_raw[ROWS:P], in_=k_rows[:, :, PASS:N])
        q_rows = qT.rearrange("(b h) (p j) n -> b (h p) j n", h=2, j=PACK)
        q_raw = {}
        for name, pair, q0, width in (("qa", 0, 0, HALF), ("qb", 0, HALF, HALF)):
            q_raw[name] = tile(name + "_raw", [P, PACK, width], F32)
            nc.sync.dma_start(out=q_raw[name][:], in_=q_rows[pair, :, :, q0 : q0 + width])
        v_raw = tile("v_raw", [P, 2, PACK, E], F32)
        nc.sync.dma_start(out=v_raw[:], in_=v[0].rearrange("(g p j) e -> p g j e", g=2, j=PACK))
        q_raw["qc"] = tile("qc_raw", [P, PACK, NQ], F32)
        nc.sync.dma_start(out=q_raw["qc"][:], in_=q_rows[1])

        k_own = tile("k_own", [P, PASS + PASS // 4], I32)
        k_other = tile("k_other", [P, PASS + PASS // 4], I32)
        nc.gpsimd.memset(k_own[:, PASS:], 0)

        t_flat = t_sb[:].rearrange("p g j -> p (g j)")
        t_abs = tile("t_abs", [P, 8], F32)
        ln_in = tile("ln_in", [P, 16], F32)
        t_rec = tile("t_rec", [P, 8], F32)
        t_sign = tile("t_sign", [P, 8], F32)
        ln_out = tile("ln_out", [P, 16], F32)
        ln_t = tile("ln_t", [P, 8], F32)
        nc.vector.scalar_tensor_tensor(out=t_abs[:], in0=t_flat, scalar=-1.0, in1=t_flat, op0=ALU.mult, op1=ALU.max)
        nc.vector.tensor_scalar(out=ln_in[:, 0:8], in0=t_abs[:], scalar1=LN_MIN, scalar2=LN_MAX, op0=ALU.max, op1=ALU.min)
        nc.vector.reciprocal(out=t_rec[:], in_=ln_in[:, 0:8])
        nc.vector.scalar_tensor_tensor(out=ln_in[:, 8:16], in0=t_abs[:], scalar=F32_MIN, in1=t_rec[:], op0=ALU.max, op1=ALU.mult)
        nc.scalar.activation(out=ln_out[:], in_=ln_in[:], func=ACT.Ln)
        nc.scalar.activation(out=t_sign[:], in_=t_flat, func=ACT.Sign)

        k_grouped = tile("k_grouped", [P, PASS * PACK], BF16)
        nc.vector.tensor_copy(
            out=k_grouped[:].rearrange("p (r s j) -> p s j r", r=PACK, j=PACK),
            in_=k_raw[:].rearrange("p j (s r) -> p s j r", r=PACK),
        )
        nc.vector.tensor_tensor(out=ln_t[:], in0=ln_out[:, 0:8], in1=ln_out[:, 8:16], op=ALU.add)
        q_grouped = {"qa": interleave("qa", q_raw["qa"][:], HALF)}
        nc.vector.quantize_mx(out=k_own[:, 0:PASS].bitcast(FP8X4), scales=k_own[:, PASS:].bitcast(U8), in_=k_grouped[:])
        q_mx = {"qa": quantize("qa", q_grouped["qa"], HALF)}

        def swap_k():
            nc.scalar.dma_start(out=k_other[0:ROWS, :], in_=k_own[ROWS:P, :])
            nc.scalar.dma_start(out=k_other[ROWS:P, :], in_=k_own[0:ROWS, :])

        v_grouped = tile("v_grouped", [P, 2 * E * PACK], BF16)
        v_mx = {}

        def group_q(name, width):
            q_grouped[name] = interleave(name, q_raw[name][:], width)

        def quantize_q(name, width):
            q_mx[name] = quantize(name, q_grouped[name], width)

        def group_v(g):
            nc.vector.tensor_tensor(
                out=v_grouped[:, g * PASS : (g + 1) * PASS].rearrange("p (c i j) -> p c j i", i=4, j=PACK),
                in0=v_raw[:, g].rearrange("p j (c i) -> p c j i", i=4),
                in1=t_sign[:, g * PACK : (g + 1) * PACK].unsqueeze(1).unsqueeze(3).to_broadcast([P, E // 4, PACK, 4]),
                op=ALU.mult,
            )

        def quantize_v():
            v_mx["v"] = quantize("v", v_grouped[:], 2 * E)

        def q_source(h, q0):
            if h >= 2:
                return "qc", q0
            return ("qa", q0) if q0 < HALF else ("qb", q0 - HALF)

        units = []
        for q0 in (0, HALF):
            units.extend([(0, 0, q0, HALF), (1, 1, q0, HALF)])
        units.extend([(0, 1, 0, NQ), (1, 0, 0, NQ), (2, 0, 0, NQ), (3, 1, 0, NQ)])
        units.extend([(2, 1, 0, HALF), (3, 0, 0, HALF), (2, 1, HALF, HALF)])
        if TAIL:
            units.extend([(3, 0, HALF, COLS), (3, 0, HALF + COLS, COLS)])
        else:
            units.append((3, 0, HALF, HALF))
        fills = []
        for unit in units:
            per_bank = NQ // unit[3]
            fills.extend([(unit, first, per_bank) for first in range(0, PACK, per_bank)])

        def row_tile(i):
            return fills[i][0][0] % 2

        groups, taken = [], set()
        for i in range(len(fills)):
            if i not in taken:
                mates = [j for j in range(i + 1, min(i + 3, len(fills))) if j not in taken and row_tile(j) != row_tile(i)]
                groups.append([i] + mates[-1:])
                for j in groups[-1]:
                    taken.add(j)

        def frees(i):
            earlier = [j for j in range(i) if row_tile(j) == row_tile(i)]
            return earlier[-SCORE_BANKS] if len(earlier) >= SCORE_BANKS else -1

        banks, weights, w_mx = {}, {}, {}

        def scores(group):
            calls = []
            for i in group:
                (h, g, q0, width), first_r, count = fills[i]
                T = row_tile(i)
                banks[i] = score_pools[T].tile([P, NQ], F32, name="bank%d" % T)
                k_mx = k_own if g == T else k_other
                rows = slice(T * ROWS, (T + 1) * ROWS)
                for c in range(NQ // COLS):
                    r = first_r + c * COLS // width
                    name, first = q_source(h, q0 + c * COLS % width)
                    codes, scales = q_mx[name]
                    calls.append((c, i, dict(
                        out=banks[i][:, c * COLS : (c + 1) * COLS],
                        lhsT=k_mx[rows, r * COLS : (r + 1) * COLS].bitcast(FP8X4),
                        lhsT_scale=k_mx[rows, PASS + r * COLS // 4 : PASS + (r + 1) * COLS // 4].bitcast(U8),
                        rhs=codes[rows, first : first + COLS].bitcast(FP8X4),
                        rhs_scale=scales[rows, first : first + COLS])))
            for c, i, operands in sorted(calls, key=lambda call: call[:2]):
                nc.tensor.matmul_mx(start=True, stop=True, **operands)

        def name_of(unit):
            return "w%d_%d_%d" % unit[:3]

        def exps(i):
            unit, first_r, count = fills[i]
            h, g, q0, width = unit
            if first_r == 0:
                weights[unit] = tile(name_of(unit) + "_rows", [P, PACK, width], BF16)
            for n in range(count):
                r = first_r + n
                nc.scalar.activation(out=weights[unit][:, r, :], in_=banks[i][:, n * width : (n + 1) * width], func=ACT.Exp,
                                     bias=ln_t[:, g * PACK + r : g * PACK + r + 1])
            return first_r + count == PACK

        y_banks = {}

        def values(unit):
            h, g, q0, width = unit
            y = y_pool.tile([P, NQ // COLS, E], F32, name="y")
            y_banks[unit] = y
            v_codes, v_scales = v_mx["v"]
            for c in range(width // COLS):
                q = q0 + c * COLS
                parts = [u for u in w_mx if u[0] == h and u[2] <= q < u[2] + u[3]]
                for n, u in enumerate(parts):
                    codes, scales = w_mx[u]
                    cols = slice(q - u[2], q - u[2] + COLS)
                    v_cols = slice(u[1] * E, (u[1] + 1) * E)
                    nc.tensor.matmul_mx(out=y[:, c, :], lhsT=codes[:, cols].bitcast(FP8X4), lhsT_scale=scales[:, cols],
                                        rhs=v_codes[:, v_cols].bitcast(FP8X4), rhs_scale=v_scales[:, v_cols],
                                        start=(n == 0), stop=(n == 1))

        recs = {}

        def reciprocals(unit):
            tiles = unit[3] // COLS
            recs[unit] = tile("rec" + name_of(unit), [P, tiles], F32)
            nc.vector.reciprocal(out=recs[unit][:], in_=y_banks[unit][:, 0:tiles, E - 1])

        def divide(unit):
            h, g, q0, width = unit
            tiles = width // COLS
            y, rec = y_banks[unit], recs[unit]
            result = tile("result" + name_of(unit), [P, tiles, E], F32)
            if h < VECTOR_HEADS:
                nc.vector.tensor_tensor(out=result[:], in0=y[:, 0:tiles, :], in1=rec[:].unsqueeze(2).to_broadcast([P, tiles, E]), op=ALU.mult)
            else:
                for c in range(tiles):
                    nc.scalar.activation(out=result[:, c, :], in_=y[:, c, :], func=ACT.Copy, scale=rec[:, c : c + 1])
            nc.sync.dma_start(out=out[h, q0 : q0 + width, :].rearrange("(c p) e -> p c e", p=P), in_=result[:])

        early = {}
        early.setdefault(0, []).extend([swap_k, lambda: group_q("qb", HALF), lambda: quantize_q("qb", HALF)])
        early.setdefault(V_SLOT, []).extend([lambda: group_v(0), lambda: group_v(1)])
        early.setdefault(QC_SLOT, []).extend([lambda: group_q("qc", NQ), quantize_v, lambda: quantize_q("qc", NQ)])
        divisions = {}

        def closes(n):
            return 0 <= n < len(units) and units[n][1] != units[n][0] % 2

        def weights_to_mx(n, slot):
            h, g, q0, width = unit = units[n]
            parts = min(2, width // COLS)
            halves = [(h, g, q0 + m * width // parts, width // parts) for m in range(parts)]
            before = units[n - PV_UNITS] if closes(n - PV_UNITS) else None
            if before:
                values(before)
            grouped = [interleave(name_of(half), weights[unit][:, :, half[2] - q0 : half[2] - q0 + half[3]], half[3]) for half in halves]
            if before:
                reciprocals(before)
            w_mx[halves[0]] = quantize(name_of(halves[0]), grouped[0], halves[0][3])
            if before and before[0] < VECTOR_HEADS:
                divide(before)
            elif before:
                divisions.setdefault(min(slot + DIV_DELAY, len(fills) - 1), []).append(before)
            if parts == 2:
                w_mx[halves[1]] = quantize(name_of(halves[1]), grouped[1], halves[1][3])

        for slot in range(len(fills)):
            while groups and max(frees(i) for i in groups[0]) < slot and groups[0][0] <= slot + AHEAD:
                scores(groups.pop(0))
            done = exps(slot)
            for work in early.get(slot, []):
                work()
            if done:
                weights_to_mx(units.index(fills[slot][0]), slot)
            for unit in divisions.get(slot, []):
                divide(unit)
        for unit in units[-PV_UNITS:]:
            values(unit)
            reciprocals(unit)
            divide(unit)
